import numpy as np, ml_dtypes
CORES = [40,64,80,88,96,104,120,144]
N = 8
import mx_ref
BF = ml_dtypes.bfloat16
def gentries(a):
    return np.ascontiguousarray(a.reshape(8, 16, -1).transpose(0, 2, 1)).reshape(8, -1)
def gtable(e):
    e = np.asarray(e); return np.ascontiguousarray(e.reshape(8, -1, 16).transpose(0, 2, 1)).reshape(128, -1).astype(np.int32)
def gcols(t, e):
    v = np.concatenate([t.reshape(8, 16, -1, 4), np.zeros((8, 16, 1, 4), BF)], axis=2)
    return np.ascontiguousarray(np.stack([v[g][:, e[g]] for g in range(8)])).reshape(128, -1)
def gpick(z, e):
    return np.concatenate([z[16 * g:16 * g + 16][:, e[g]] for g in range(8)])
def f(rng, *shape):
    return mx_ref.flush((rng.standard_normal(shape, dtype=np.float32) * np.exp2(rng.integers(-2, 3, shape[:-1] + (1,)))).astype(BF))
def wide(rng, *shape, cols=0):
    v = rng.standard_normal(shape, dtype=np.float32) * np.exp2(rng.integers(-12, 13, shape)).astype(np.float32)
    if cols: v *= np.repeat(np.exp2(rng.integers(-cols, cols + 1, shape[:-2] + (1, shape[-1] // 4))) * (rng.random(shape[:-2] + (1, shape[-1] // 4)) > 0.0625), 4, axis=-1).astype(np.float32)
    return mx_ref.flush(v.astype(BF))
T, CAPP, NB, KK = 512, 64, 2, 256
MASK = np.repeat(np.arange(128)[:, None] // 16 == np.arange(128)[None] // 16, 4, axis=1)
def lists(rng, agree=False, one=False, full=False, repeat=False):
    a, o = [], []
    for r in range(N):
        n = rng.integers(0, CAPP + 1, (8, N))
        far, most, none = -1, -1, -1
        if one:
            far = (r + rng.integers(1, N)) % N; most, none = rng.permutation(8)[:2]
            n[most, far] = CAPP; n[none, far] = 0
        if full: n[:] = CAPP
        n[n.sum(axis=1) == 0, r] = 1
        e = np.full((8, N, CAPP), -1)
        for g in range(8):
            for q in range(N):
                v = rng.integers(0, T, n[g, q])
                if one and g == most and q == far: v = rng.permutation(T)[:CAPP]
                if full: v[0] = 0; v[1] = T - 1
                e[g, q, rng.permutation(CAPP)[:n[g, q]]] = v
        if agree: e = np.stack([e[0]] * 8)
        e = e.reshape(8, -1); used = [np.flatnonzero(e[g] >= 0) for g in range(8)]
        k = np.stack([np.full(KK, rng.choice(u)) if repeat else rng.choice(u, KK) for u in used])
        if one: k[most, rng.permutation(KK)[:CAPP]] = far * CAPP + rng.permutation(CAPP)
        if full: k[:, 0] = 0; k[:, -1] = N * CAPP - 1
        a.append(gtable(e)); o.append(gtable(k))
    return {"rq": np.stack(a), "od": np.stack(o)}
def setup_inputs(rng):
    ky = f(rng, N, 128, 4 * T); qd = np.array(f(rng, N, 128, NB * 512))
    qd[:, ~np.concatenate([MASK] * NB, axis=1)] = 0
    return {"ky": ky, "qd": qd, **lists(rng)}
def setup_inputs_agree(rng):
    return {**setup_inputs(rng), **lists(rng, agree=True)}
def setup_inputs_one(rng):
    return {**setup_inputs(rng), **lists(rng, one=True)}
def setup_inputs_full(rng):
    return {**setup_inputs(rng), **lists(rng, full=True)}
def setup_inputs_repeat(rng):
    return {**setup_inputs(rng), **lists(rng, repeat=True)}
def setup_inputs_spread(rng):
    d = setup_inputs(rng); d["ky"] = wide(rng, N, 128, 4 * T, cols=8); return d
def check_inputs(d):
    b = []
    for r in range(N):
        e, o = gentries(d["rq"][r]), gentries(d["od"][r])
        if e.min() < -1 or e.max() >= T: b.append("rq")
        if o.min() < 0 or o.max() >= N * CAPP or (np.take_along_axis(e, np.clip(o, 0, N * CAPP - 1), axis=1) < 0).any(): b.append("od")
        if not (d["qd"][r][~np.concatenate([MASK] * NB, axis=1)].astype(np.float32) == 0).all(): b.append("qd")
    return b
def reference(ky, qd, rq, od):
    y = np.zeros((N, 128, NB * KK), np.float32)
    for r in range(N):
        e, o = gentries(rq[r]), gentries(od[r])
        slots = mx_ref.quantize(np.concatenate([gcols(ky[q], e[:, q * CAPP:(q + 1) * CAPP]) for q in range(N)], axis=1))
        for b in range(NB):
            z = mx_ref.matmul(mx_ref.quantize(np.ascontiguousarray(qd[r][:, 512 * b:512 * b + 512])), slots)
            y[r][:, KK * b:KK * b + KK] = gpick(z, o)
    return {"y": y}

import comms_topo
from concourse.bass import DstId, RemoteDMATransfer
from concourse.mybir import dt, AluOpType, ActivationFunctionType

N = 8
W = 64
LC = 4
COPY = ActivationFunctionType.Copy

SCRATCH = {
    "rqi": ("sbuf", [128, 32], "int32"),
    "lst": ("sbuf", [128, 32], "uint16"),
    "offa": ("sbuf", [128, 12], "uint16"),
    "offb0": ("sbuf", [128, 8], "uint16"),
    "offb1": ("sbuf", [128, 8], "uint16"),
    "hl": ("sbuf", [128, 32], "uint16"),
    "kyt": ("sbuf", [128, 2048], "bfloat16"),
    "kp0": ("sbuf", [128, 512], "bfloat16"),
    "kp1": ("sbuf", [128, 512], "bfloat16"),
    "kp2": ("sbuf", [128, 512], "bfloat16"),
    "kp3": ("sbuf", [128, 512], "bfloat16"),
    "ta": ("sbuf", [128, 1024], "bfloat16"),
    "tb0": ("sbuf", [128, 512], "bfloat16"),
    "tb1": ("sbuf", [128, 512], "bfloat16"),
    "ca": ("sbuf", [128, 256], "float8_e4m3fn_x4"),
    "pa": ("sbuf", [128, 256], "uint8"),
    "cb0": ("sbuf", [128, 128], "float8_e4m3fn_x4"),
    "pb0": ("sbuf", [128, 128], "uint8"),
    "cb1": ("sbuf", [128, 128], "float8_e4m3fn_x4"),
    "pb1": ("sbuf", [128, 128], "uint8"),
    "hc": ("sbuf", [128, 128], "float8_e4m3fn_x4"),
    "hp": ("sbuf", [128, 128], "uint8"),
    "qt": ("sbuf", [128, 1024], "bfloat16"),
    "qc": ("sbuf", [128, 256], "float8_e4m3fn_x4"),
    "qp": ("sbuf", [128, 256], "uint8"),
    "lc": ("sbuf", [128, 448], "float8_e4m3fn_x4"),
    "lp": ("sbuf", [128, 448], "uint8"),
    "ps": ("psum", [128, 4096], "float32"),
    "z0": ("sbuf", [128, 512], "float32"),
    "z1": ("sbuf", [128, 512], "float32"),
    "odi": ("sbuf", [128, 16], "int32"),
    "om": ("sbuf", [128, 128], "float32"),
    "om2": ("sbuf", [128, 64], "float32"),
    "om3": ("sbuf", [128, 32], "float32"),
    "om4": ("sbuf", [128, 16], "float32"),
    "offo": ("sbuf", [128, 16], "uint16"),
    "y0": ("sbuf", [128, 256], "float32"),
    "y1": ("sbuf", [128, 256], "float32"),
}
SEMAPHORES = [
    "d_rq", "d_ky", "d_qd", "d_od", "d_y0", "d_y1",
    "v_lst", "v_kp", "s_kp",
    "v_go", "s_go", "v_ga", "s_ga", "v_gb0", "s_gb0", "v_gb1", "s_gb1",
    "q_a", "q_b0", "q_b1", "q_q",
    "o_1", "o_2", "o_3", "o_4", "o_5",
    "t0_0", "t0_1", "t0_2", "t0_3", "t1_0", "t1_1", "t1_2", "t1_3",
    "v_z", "s_z", "v_y", "s_y",
    "la", "lb0", "lb1", "ra", "rb0", "rb1", "sent",
    "h_l", "h_c", "h_p", "h_sent",
]


def order(core, T, topo):
    me = T.rank_of(core)
    cores = list(T.cores)
    direct = [q for q in range(N) if q != me and topo.may_write(core, cores[q])]
    cross = [q for q in range(N) if q != me and q not in direct]
    j = sorted([me] + direct).index(me)
    p0 = [q for i, q in enumerate(cross) if i // 2 == j // 2]
    p1 = [q for i, q in enumerate(cross) if i // 2 != j // 2]
    return [me] + direct + p0 + p1


def helpers(core, T, topo):
    o = order(core, T, topo)
    cross = [list(T.cores)[q] for q in o[4:]]
    ok = [h for h in topo.cores_of(core) if h != core and all(topo.may_write(h, d) for d in cross)]
    return [[h for h in ok if topo.die(h) == topo.die(core)][0], [h for h in ok if topo.die(h) != topo.die(core)][0]]


def runs(o):
    n = max(max(o[4:6]) - min(o[4:6]), max(o[6:8]) - min(o[6:8])) + 1
    return [min(min(o[4:6]), N - n), min(min(o[6:8]), N - n)], n


def bits(es):
    return sum(1 << e for e in es)


def dst_id(topo, dst, src):
    rid, pid = topo.addr(dst, src)
    return DstId(rid=rid, pnc=pid)


def helper_program(g, core, T, topo, owner, k):
    cores = list(T.cores)
    me = T.rank_of(owner)
    o = order(owner, T, topo)
    pair = o[4 + 2 * k:6 + 2 * k]
    first, n = runs(o)
    inner = topo.engines(owner, core)
    n_in = len([e for e in inner if e not in topo.engines(core, cores[pair[0]])])
    sent = 0

    def send(pieces):
        tr = []
        for i, (q, src, dst, sem) in enumerate(pieces):
            es = topo.engines(core, cores[q])
            h = len(es) // 2
            tr.append(RemoteDMATransfer(dst_ids=[dst_id(topo, cores[q], core)], dma_engine_mask=bits(es[i * h:i * h + h]),
                                        remote_sem=sem, src=src, dst=dst))
        g.remote_dma_fused(tr, local_sem=T.sem.h_sent)
        return 2 * h

    seat = [order(cores[q], T, topo).index(me) for q in pair]
    g.wait_ge(T.sem.h_l, n_in // 2)
    sent += send([(q, T.hl[:, LC * (q - first[k]):LC * (q - first[k]) + LC],
                   T["offb%d" % k][:, LC * (s - 4 - 2 * k):LC * (s - 4 - 2 * k) + LC], T.sem["lb%d" % k])
                  for q, s in zip(pair, seat)])
    g.wait_ge(T.sem.h_c, n_in)
    sent += send([(q, T.hc[:, W * i:W * i + W].bitcast(dt.uint8),
                   T.lc[:, W * (s - 1):W * s].bitcast(dt.uint8), T.sem["rb%d" % k])
                  for i, (q, s) in enumerate(zip(pair, seat))])
    g.wait_ge(T.sem.h_p, n_in)
    sent += send([(q, T.hp[:, W * i:W * i + W], T.lp[:, W * (s - 1):W * s], T.sem["rb%d" % k])
                  for i, (q, s) in enumerate(zip(pair, seat))])
    g.wait_ge(T.sem.h_sent, sent)


def rank_program(g, core, T, topo):
    cores = list(T.cores)
    rank = T.rank_of(core)
    if rank is None:
        for owner in cores:
            if core in topo.cores_of(owner):
                hs = helpers(owner, T, topo)
                if core in hs:
                    helper_program(g, core, T, topo, owner, hs.index(core))
        return

    o = order(core, T, topo)
    hs = helpers(core, T, topo)
    seat = [order(cores[q], T, topo).index(rank) for q in o]
    out_es = topo.engines(core, cores[o[1]])
    in_es = [e for e in topo.engines(core, hs[0]) if e not in out_es]
    S = T.sem

    g.sync.dma_start(T.rqi[:], T.rq[:]).then_inc(S.d_rq, 16)
    g.sync.dma_start(T.kyt[:, 0:1024], T.ky[:, 0:1024]).then_inc(S.d_ky, 16)
    g.sync.wait_ge(S.la, 6)
    g.sync.dma_start(T.qt[:], T.qd[:]).then_inc(S.d_qd, 16)
    g.sync.dma_start(T.odi[:], T.od[:]).then_inc(S.d_od, 16)
    g.sync.wait_ge(S.v_y, 1)
    g.sync.dma_start(T.y[:, 0:256], T.y0[:]).then_inc(S.d_y0, 16)
    g.sync.wait_ge(S.d_y0, 16)

    sent = 0

    def fused(trs, engines):
        g.remote_dma_fused(trs, local_sem=S.sent)
        return engines

    first, n = runs(o)
    g.wait_ge(S.v_lst, 1)
    hq = len(in_es) // 2
    sent += fused([RemoteDMATransfer(dst_ids=[dst_id(topo, hs[k], core)], dma_engine_mask=bits(in_es[k * hq:k * hq + hq]),
                                     remote_sem=S.h_l, src=T.lst[:, LC * first[k]:LC * (first[k] + n)],
                                     dst=T.hl[:, 0:LC * n]) for k in range(2)], 2 * hq)

    def direct(src, dst, sem):
        trs = []
        for i in range(1, 4):
            d = cores[o[i]]
            trs.append(RemoteDMATransfer(dst_ids=[dst_id(topo, d, core)],
                                         dma_engine_mask=bits(topo.engines(core, d)[2 * (i - 1):2 * i]),
                                         remote_sem=sem, src=src(i), dst=dst(i)))
        return fused(trs, 6)

    sent += direct(lambda i: T.lst[:, LC * o[i]:LC * o[i] + LC],
                   lambda i: T.offa[:, LC * (seat[i] - 1):LC * seat[i]], S.la)
    g.wait_ge(S.q_a, 1)
    sent += direct(lambda i: T.ca[:, W * i:W * i + W].bitcast(dt.uint8),
                   lambda i: T.lc[:, W * (seat[i] - 1):W * seat[i]].bitcast(dt.uint8), S.ra)
    sent += direct(lambda i: T.pa[:, W * i:W * i + W], lambda i: T.lp[:, W * (seat[i] - 1):W * seat[i]], S.ra)
    for k in range(2):
        rid, pid = topo.addr(hs[k], core)
        g.wait_ge(S["q_b%d" % k], 1)
        g.remote_dma(T.hc[:].bitcast(dt.uint8), T["cb%d" % k][:].bitcast(dt.uint8), S.h_c, S.sent, pid, rid, bits(in_es))
        g.remote_dma(T.hp[:], T["pb%d" % k][:], S.h_p, S.sent, pid, rid, bits(in_es))
        sent += 2 * len(in_es)
    g.wait_ge(S.sent, sent)

    v, sc, pe = g.vector, g.scalar, g.tensor
    v.wait_ge(S.d_rq, 16)
    v.tensor_copy(T.lst[:], T.rqi[:]).then_inc(S.v_lst, 1)
    v.wait_ge(S.d_ky, 32)
    for t in range(3):
        v.tensor_copy(T["kp%d" % t][:], T.kyt[:, t:2048:4]).then_inc(S.v_kp, 1)

    sc.dma_start(T.kyt[:, 1024:2048], T.ky[:, 1024:2048]).then_inc(S.d_ky, 16)
    sc.wait_ge(S.d_ky, 32)
    sc.activation(T.kp3[:], T.kyt[:, 3:2048:4], COPY).then_inc(S.s_kp, 1)

    v.wait_ge(S.v_kp, 3)
    v.wait_ge(S.v_lst, 1)
    sc.wait_ge(S.v_kp, 3)
    sc.wait_ge(S.v_lst, 1)
    sc.wait_ge(S.s_kp, 1)

    def gather(tile, a, b, offs, name):
        for t in range(4):
            out = T[tile][:, 4 * a + t:4 * b:4]
            src = T["kp%d" % t][:, 0:512].indirect(offs)
            if t < 2:
                v.tensor_copy(out, src).then_inc(S["v_g" + name], 1)
            else:
                sc.activation(out, src, COPY).then_inc(S["s_g" + name], 1)

    gather("ta", 0, W, T.lst[:, LC * rank:LC * rank + LC], "o")
    v.wait_ge(S.la, 6)
    sc.wait_ge(S.la, 6)
    gather("ta", W, 4 * W, T.offa[:, 0:12], "a")
    for s in ("v_go", "s_go", "v_ga", "s_ga"):
        v.wait_ge(S[s], 2)
    v.quantize_mx(T.ca[:], T.pa[:], T.ta[:]).then_inc(S.q_a, 1)
    for k in range(2):
        v.wait_ge(S["lb%d" % k], 8)
        sc.wait_ge(S["lb%d" % k], 8)
        gather("tb%d" % k, 0, 2 * W, T["offb%d" % k][:, 0:8], "b%d" % k)
        v.wait_ge(S["v_gb%d" % k], 2)
        v.wait_ge(S["s_gb%d" % k], 2)
        v.quantize_mx(T["cb%d" % k][:], T["pb%d" % k][:], T["tb%d" % k][:]).then_inc(S["q_b%d" % k], 1)

    v.wait_ge(S.d_qd, 16)
    v.quantize_mx(T.qc[:], T.qp[:], T.qt[:]).then_inc(S.q_q, 1)
    v.wait_ge(S.d_od, 16)
    shift = [W * (o.index(q) - q) for q in range(N)]
    v.tensor_scalar(T.om[:, 0:16], T.odi[:], float(shift[0]), None, AluOpType.add).then_inc(S.o_1, 1)
    for q in range(1, N):
        v.tensor_scalar(T.om[:, 16 * q:16 * q + 16], T.odi[:], float(W * q), float(shift[q] - shift[q - 1]),
                        AluOpType.is_ge, AluOpType.mult).then_inc(S.o_1, 1)
    v.wait_ge(S.o_1, 8)
    v.tensor_tensor(T.om2[:], T.om[:, 0:64], T.om[:, 64:128], AluOpType.add).then_inc(S.o_2, 1)
    v.wait_ge(S.o_2, 1)
    v.tensor_tensor(T.om3[:], T.om2[:, 0:32], T.om2[:, 32:64], AluOpType.add).then_inc(S.o_3, 1)
    v.wait_ge(S.o_3, 1)
    v.tensor_tensor(T.om4[:], T.om3[:, 0:16], T.om3[:, 16:32], AluOpType.add).then_inc(S.o_4, 1)
    v.wait_ge(S.o_4, 1)
    v.tensor_copy(T.offo[:], T.om4[:]).then_inc(S.o_5, 1)

    pieces = [("ca", "pa", 0, 2 * W), ("lc", "lp", 0, 3 * W), ("lc", "lp", 3 * W, 5 * W), ("lc", "lp", 5 * W, 7 * W)]
    ready = [[("q_a", 1), ("q_q", 1)], [("ra", 12)], [("rb0", 16)], [("rb1", 16)]]
    for j, (c, p, a, b) in enumerate(pieces):
        for s, cnt in ready[j]:
            pe.wait_ge(S[s], cnt)
        for t in range(2):
            bank = 512 * (4 * t + j)
            pe.matmul_mx(T.ps[:, bank:bank + b - a], T.qc[:, 128 * t:128 * t + 128], T.qp[:, 128 * t:128 * t + 128],
                         T[c][:, a:b], T[p][:, a:b], True, True).then_inc(S["t%d_%d" % (t, j)], 1)

    at = [0, W, 4 * W, 6 * W, 8 * W]
    for j in range(4):
        w = at[j + 1] - at[j]
        v.wait_ge(S["t0_%d" % j], 1)
        v.tensor_copy(T.z0[:, at[j]:at[j + 1]], T.ps[:, 512 * j:512 * j + w]).then_inc(S.v_z, 1)
        sc.wait_ge(S["t1_%d" % j], 1)
        sc.activation(T.z1[:, at[j]:at[j + 1]], T.ps[:, 512 * (4 + j):512 * (4 + j) + w], COPY).then_inc(S.s_z, 1)
    v.wait_ge(S.o_5, 1)
    v.wait_ge(S.v_z, 4)
    v.tensor_copy(T.y0[:], T.z0[:, 0:512].indirect(T.offo[:, 0:16])).then_inc(S.v_y, 1)
    sc.wait_ge(S.o_5, 1)
    sc.wait_ge(S.s_z, 4)
    sc.activation(T.y1[:], T.z1[:, 0:512].indirect(T.offo[:, 0:16]), COPY).then_inc(S.s_y, 1)
    sc.wait_ge(S.s_y, 1)
    sc.dma_start(T.y[:, 256:512], T.y1[:]).then_inc(S.d_y1, 16)
    sc.wait_ge(S.d_y1, 16)
